import numpy as np
import ml_dtypes


def mxq(x, axis, fmt="e4m3"):
    dtype, down = {"e4m3": (ml_dtypes.float8_e4m3fn, 7), "e5m2": (ml_dtypes.float8_e5m2, 14)}[fmt]
    v = np.moveaxis(np.asarray(x, np.float32).astype(ml_dtypes.bfloat16).astype(np.float64), axis, -1)
    blocks = v.reshape(v.shape[:-1] + (-1, 32))
    amax = np.abs(blocks).max(-1, keepdims=True)
    byte = np.maximum(np.where(amax > 0, np.frexp(amax)[1] - 1 + 127, 0) - down, 1)
    scale = np.exp2(byte - 127.0)
    codes = (blocks / scale).astype(np.float32).astype(dtype).astype(np.float64)
    return np.moveaxis((codes * scale).reshape(v.shape), -1, axis)


WIDE = False


def mx_kscale(k, group=512):
    if not WIDE:
        return np.ones(k)
    levels = np.array([10, -10, 5, -5, 0])
    if group != 512:
        return np.exp2(np.random.permutation(np.resize(levels, k // group))).repeat(group)
    if k % 512:
        return np.exp2(np.random.permutation(np.resize(levels, k // 32))).repeat(32)
    a = np.empty((k // 512, 16))
    for p in range(k // 512):
        a[p, :8] = np.random.permutation(np.resize(levels, 8))
        for g in range(8):
            far = levels[np.abs(levels - a[p, g]) >= 10]
            a[p, g + 8] = far[np.random.randint(len(far))]
    return np.exp2(a.ravel()).repeat(32)


def f64(x):
    return np.asarray(x).astype(np.float64)


G, D, M, N = 2, 256, 128, 512


def setup_inputs():
    n = np.random.standard_normal
    s_d = mx_kscale(D, 0)
    return {
        "x": (n((G, D, M)) / s_d[:, None] / np.sqrt(D)).astype(np.float32),
        "c": (n((G, D, N)) * s_d[:, None] / np.sqrt(D)).astype(np.float32),
        "xn": (np.random.uniform(0.9, 1.3, (G, M, 1))).astype(np.float32),
        "cn": (np.random.uniform(0.9, 1.3, (G, 1, N))).astype(np.float32),
    }


def reference(x, c, xn, cn):
    xq = mxq(f64(x), 1, "e4m3")
    cq = mxq(f64(c), 1, "e4m3")
    z = xq.transpose(0, 2, 1) @ cq
    d2 = f64(xn) + f64(cn) - 2.0 * z
    y = np.exp((-1.5) * np.sqrt(d2))
    return y

@@ -1,0 +1,165 @@
+from contextlib import ExitStack
+
+import concourse.mybir as mybir
+
+G, D, M, N = 2, 256, 128, 512
+FLOPS = 2 * G * D * M * N
+
+F32 = mybir.dt.float32
+BF16 = mybir.dt.bfloat16
+U32 = mybir.dt.uint32
+U8 = mybir.dt.uint8
+FP8X4 = mybir.dt.float8_e4m3fn_x4
+ACT = mybir.ActivationFunctionType
+ALU = mybir.AluOpType
+
+P = 128
+PACK = 4
+ROWS = D // PACK
+SQ = 32
+HALF = N // 2
+CHUNK = 128
+RUN = 4
+
+
+def tile_rows_kern_laplace_kernel(tc, x, c, xn, cn, out):
+    nc = tc.nc
+    with ExitStack() as ctx:
+        sb = ctx.enter_context(tc.tile_pool(name="sb", bufs=1))
+        ps = ctx.enter_context(tc.psum_pool(name="ps", bufs=1))
+        ctx.enter_context(tc.manual_schedule())
+
+        x_raw = sb.tile([P, PACK, M], F32, name="x_raw", align_bytes=64)
+        c_raw = [sb.tile([P, PACK, HALF], F32, name="c_raw%d" % h, align_bytes=64) for h in range(2)]
+        cn_rows = sb.tile([P, SQ], F32, name="cn_rows", align_bytes=64)
+        cn_cols = sb.tile([P, SQ], F32, name="cn_cols", align_bytes=64)
+        cn_rep = [sb.tile([P, G * HALF], F32, name="cn_rep%d" % h, align_bytes=64) for h in range(2)]
+        cn_all = [sb.tile([P, G * HALF], F32, name="cn_all%d" % h, align_bytes=64) for h in range(2)]
+        xn_col = sb.tile([P, G], F32, name="xn_col")
+        warm = sb.tile([P, 1], F32, name="warm")
+        warm_out = sb.tile([P, 1], F32, name="warm_out")
+        x_bf = sb.tile([P, M * PACK], BF16, name="x_bf", align_bytes=64)
+        x_codes = sb.tile([P, M], U32, name="x_codes", align_bytes=64)
+        x_scales = sb.tile([P, M], U8, name="x_scales", align_bytes=64)
+        chunks = range(N // CHUNK)
+        c_bf = [sb.tile([P, CHUNK * PACK], BF16, name="c_bf%d" % k, align_bytes=64) for k in chunks]
+        c_codes = [sb.tile([P, CHUNK], U32, name="c_codes%d" % k, align_bytes=64) for k in chunks]
+        c_scales = [sb.tile([P, CHUNK], U8, name="c_scales%d" % k, align_bytes=64) for k in chunks]
+        z = [[ps.tile([P, CHUNK], F32, name="z%d_%d" % (g, k)) for k in chunks] for g in range(G)]
+        d2 = sb.tile([P, G * N], F32, name="d2", align_bytes=64)
+        dist = sb.tile([P, G * N], F32, name="dist", align_bytes=64)
+        y = sb.tile([P, G * N], F32, name="y", align_bytes=64)
+
+        c_rows = c.rearrange("g (p j) n -> (g p) j n", j=PACK)
+
+        def load_x(q):
+            q.dma_start(out=x_raw[:], in_=x.rearrange("g (p j) m -> (g p) j m", j=PACK))
+
+        def load_c(q, h):
+            q.dma_start(out=c_raw[h][:], in_=c_rows[:, :, h * HALF : (h + 1) * HALF])
+
+        def load_cn(q):
+            q.dma_start(
+                out=cn_rows[:],
+                in_=cn.rearrange("g o (b i) -> o (g b) i", i=SQ).to_broadcast([P // SQ, SQ, SQ]),
+            )
+
+        def load_xn(q):
+            with nc.allow_non_contiguous_dma(reason="one squared length a partition"):
+                q.dma_start(out=xn_col[:], in_=xn.rearrange("g m o -> m (g o)"))
+
+        def interleave(copy, dst, src):
+            copy(
+                out=dst.rearrange("p (w i t) -> p w t i", i=RUN, t=PACK),
+                in_=src.rearrange("p t (w i) -> p w t i", i=RUN),
+            )
+
+        def interleave_c(copy, k, lo=0, hi=CHUNK):
+            h, first = divmod(k * CHUNK, HALF)
+            interleave(copy, c_bf[k][:, lo * PACK : hi * PACK], c_raw[h][:, :, first + lo : first + hi])
+
+        def quantize(codes, scales, src):
+            nc.vector.quantize_mx(out=codes[:].bitcast(FP8X4), scales=scales[:], in_=src[:])
+
+        def quantize_c(k):
+            quantize(c_codes[k], c_scales[k], c_bf[k])
+            for g in range(G):
+                rows = slice(g * ROWS, (g + 1) * ROWS)
+                nc.tensor.matmul_mx(
+                    out=z[g][k][:],
+                    lhsT=x_codes[rows, :].bitcast(FP8X4),
+                    lhsT_scale=x_scales[rows, :],
+                    rhs=c_codes[k][rows, :].bitcast(FP8X4),
+                    rhs_scale=c_scales[k][rows, :],
+                    start=True,
+                    stop=True,
+                )
+
+        def repeat_cn(copy, h):
+            per = HALF // SQ
+            copy(
+                out=cn_rep[h][:].rearrange("p (g b r) -> p g b r", g=G, r=SQ),
+                in_=cn_cols[:].rearrange("p (g h b) -> p g h b", g=G, h=2)[:, :, h, :].unsqueeze(3).to_broadcast([P, G, per, SQ]),
+            )
+
+        def spread_cn(h):
+            nc.vector.transpose(out=cn_all[h][:], in_=cn_rep[h][:])
+
+        def squared(k, g):
+            h, first = divmod(k * CHUNK, HALF)
+            nc.vector.scalar_tensor_tensor(
+                out=d2[:, g * N + k * CHUNK : g * N + (k + 1) * CHUNK],
+                in0=z[g][k][:],
+                scalar=-2.0,
+                in1=cn_all[h][:, g * HALF + first : g * HALF + first + CHUNK],
+                op0=ALU.mult,
+                op1=ALU.add,
+            )
+
+        def root(g, lo, hi):
+            cols = slice(g * N + lo, g * N + hi)
+            nc.scalar.activation(out=dist[:, cols], in_=d2[:, cols], func=ACT.Sqrt, bias=xn_col[:, g : g + 1])
+
+        def finish(q, g, lo, hi):
+            cols = slice(g * N + lo, g * N + hi)
+            nc.scalar.activation(out=y[:, cols], in_=dist[:, cols], func=ACT.Exp, scale=-1.5)
+            q.dma_start(out=out[g, :, lo:hi], in_=y[:, cols])
+
+        vcopy = nc.vector.tensor_copy
+        scopy = nc.scalar.copy
+
+        load_cn(nc.scalar)
+        load_x(nc.sync)
+        load_c(nc.sync, 0)
+        load_c(nc.sync, 1)
+        load_xn(nc.sync)
+        nc.vector.memset(warm[:], 1.0)
+        nc.scalar.activation(out=warm_out[:], in_=warm[:], func=ACT.Sqrt)
+        nc.vector.transpose(out=cn_cols[:], in_=cn_rows[:])
+        interleave(scopy, x_bf[:], x_raw[:])
+        repeat_cn(vcopy, 0)
+        repeat_cn(scopy, 1)
+        spread_cn(0)
+        quantize(x_codes, x_scales, x_bf)
+        spread_cn(1)
+        interleave_c(scopy, 0)
+        quantize_c(0)
+        interleave_c(scopy, 1)
+        interleave_c(vcopy, 2)
+        quantize_c(1)
+        interleave_c(scopy, 3)
+        squared(0, 0)
+        squared(0, 1)
+        quantize_c(2)
+        quantize_c(3)
+        for k in range(1, 4):
+            squared(k, 0)
+            squared(k, 1)
+        for g in range(G):
+            root(g, 0, 256)
+        for k in range(2, 4):
+            for g in range(G):
+                root(g, k * CHUNK, (k + 1) * CHUNK)
+        for g in range(G):
+            for h in range(2):
+                finish(nc.sync, g, h * HALF, (h + 1) * HALF)

@@ -19,7 +19,7 @@ ROWS = D // PACK
 SQ = 32
 HALF = N // 2
 CHUNK = 128
-RUN = 4
+RUN = 2
 
 
 def tile_rows_kern_laplace_kernel(tc, x, c, xn, cn, out):
@@ -30,7 +30,8 @@ def tile_rows_kern_laplace_kernel(tc, x, c, xn, cn, out):
         ctx.enter_context(tc.manual_schedule())
 
         x_raw = sb.tile([P, PACK, M], F32, name="x_raw", align_bytes=64)
-        c_raw = [sb.tile([P, PACK, HALF], F32, name="c_raw%d" % h, align_bytes=64) for h in range(2)]
+        loads = [(0, 256), (256, 512)]
+        c_raw = [sb.tile([P, PACK, hi - lo], F32, name="c_raw%d" % lo, align_bytes=64) for lo, hi in loads]
         cn_rows = sb.tile([P, SQ], F32, name="cn_rows", align_bytes=64)
         cn_cols = sb.tile([P, SQ], F32, name="cn_cols", align_bytes=64)
         cn_rep = [sb.tile([P, G * HALF], F32, name="cn_rep%d" % h, align_bytes=64) for h in range(2)]
@@ -45,7 +46,13 @@ def tile_rows_kern_laplace_kernel(tc, x, c, xn, cn, out):
         c_bf = [sb.tile([P, CHUNK * PACK], BF16, name="c_bf%d" % k, align_bytes=64) for k in chunks]
         c_codes = [sb.tile([P, CHUNK], U32, name="c_codes%d" % k, align_bytes=64) for k in chunks]
         c_scales = [sb.tile([P, CHUNK], U8, name="c_scales%d" % k, align_bytes=64) for k in chunks]
-        z = [[ps.tile([P, CHUNK], F32, name="z%d_%d" % (g, k)) for k in chunks] for g in range(G)]
+        spans = [(0, 128), (128, 256), (256, 384), (384, 512)]
+        banks = [[ps.tile([P, hi - lo], F32, name="z%d_%d" % (g, lo)) for lo, hi in spans] for g in range(G)]
+
+        def z_view(g, lo, hi):
+            s = [i for i in range(len(spans)) if spans[i][0] <= lo < spans[i][1]][0]
+            return banks[g][s][:, lo - spans[s][0] : hi - spans[s][0]]
+
         d2 = sb.tile([P, G * N], F32, name="d2", align_bytes=64)
         dist = sb.tile([P, G * N], F32, name="dist", align_bytes=64)
         y = sb.tile([P, G * N], F32, name="y", align_bytes=64)
@@ -56,7 +63,7 @@ def tile_rows_kern_laplace_kernel(tc, x, c, xn, cn, out):
             q.dma_start(out=x_raw[:], in_=x.rearrange("g (p j) m -> (g p) j m", j=PACK))
 
         def load_c(q, h):
-            q.dma_start(out=c_raw[h][:], in_=c_rows[:, :, h * HALF : (h + 1) * HALF])
+            q.dma_start(out=c_raw[h][:], in_=c_rows[:, :, loads[h][0] : loads[h][1]])
 
         def load_cn(q):
             q.dma_start(
@@ -75,7 +82,8 @@ def tile_rows_kern_laplace_kernel(tc, x, c, xn, cn, out):
             )
 
         def interleave_c(copy, k, lo=0, hi=CHUNK):
-            h, first = divmod(k * CHUNK, HALF)
+            h = [i for i in range(len(loads)) if loads[i][0] <= k * CHUNK < loads[i][1]][0]
+            first = k * CHUNK - loads[h][0]
             interleave(copy, c_bf[k][:, lo * PACK : hi * PACK], c_raw[h][:, :, first + lo : first + hi])
 
         def quantize(codes, scales, src):
@@ -86,7 +94,7 @@ def tile_rows_kern_laplace_kernel(tc, x, c, xn, cn, out):
             for g in range(G):
                 rows = slice(g * ROWS, (g + 1) * ROWS)
                 nc.tensor.matmul_mx(
-                    out=z[g][k][:],
+                    out=z_view(g, k * CHUNK, (k + 1) * CHUNK),
                     lhsT=x_codes[rows, :].bitcast(FP8X4),
                     lhsT_scale=x_scales[rows, :],
                     rhs=c_codes[k][rows, :].bitcast(FP8X4),
@@ -95,23 +103,23 @@ def tile_rows_kern_laplace_kernel(tc, x, c, xn, cn, out):
                     stop=True,
                 )
 
-        def repeat_cn(copy, h):
+        def repeat_cn(copy, h, g0=0, g1=G):
             per = HALF // SQ
             copy(
-                out=cn_rep[h][:].rearrange("p (g b r) -> p g b r", g=G, r=SQ),
-                in_=cn_cols[:].rearrange("p (g h b) -> p g h b", g=G, h=2)[:, :, h, :].unsqueeze(3).to_broadcast([P, G, per, SQ]),
+                out=cn_rep[h][:, g0 * HALF : g1 * HALF].rearrange("p (g b r) -> p g b r", b=per, r=SQ),
+                in_=cn_cols[:].rearrange("p (g h b) -> p g h b", g=G, h=2)[:, g0:g1, h, :].unsqueeze(3).to_broadcast([P, g1 - g0, per, SQ]),
             )
 
-        def spread_cn(h):
-            nc.vector.transpose(out=cn_all[h][:], in_=cn_rep[h][:])
+        def spread_cn(h, g0=0, g1=G):
+            nc.vector.transpose(out=cn_all[h][:, g0 * HALF : g1 * HALF], in_=cn_rep[h][:, g0 * HALF : g1 * HALF])
 
-        def squared(k, g):
-            h, first = divmod(k * CHUNK, HALF)
+        def squared(g, lo, hi):
+            h, first = divmod(lo, HALF)
             nc.vector.scalar_tensor_tensor(
-                out=d2[:, g * N + k * CHUNK : g * N + (k + 1) * CHUNK],
-                in0=z[g][k][:],
+                out=d2[:, g * N + lo : g * N + hi],
+                in0=z_view(g, lo, hi),
                 scalar=-2.0,
-                in1=cn_all[h][:, g * HALF + first : g * HALF + first + CHUNK],
+                in1=cn_all[h][:, g * HALF + first : g * HALF + first + hi - lo],
                 op0=ALU.mult,
                 op1=ALU.add,
             )
@@ -125,41 +133,47 @@ def tile_rows_kern_laplace_kernel(tc, x, c, xn, cn, out):
             nc.scalar.activation(out=y[:, cols], in_=dist[:, cols], func=ACT.Exp, scale=-1.5)
             q.dma_start(out=out[g, :, lo:hi], in_=y[:, cols])
 
+        def squares(k):
+            for g in range(G):
+                squared(g, k * CHUNK, (k + 1) * CHUNK)
+
+        def roots(lo, hi):
+            for g in range(G):
+                root(g, lo, hi)
+
         vcopy = nc.vector.tensor_copy
         scopy = nc.scalar.copy
 
-        load_cn(nc.scalar)
+        load_cn(nc.sync)
         load_x(nc.sync)
-        load_c(nc.sync, 0)
-        load_c(nc.sync, 1)
-        load_xn(nc.sync)
+        for h in range(len(loads)):
+            load_c(nc.sync, h)
         nc.vector.memset(warm[:], 1.0)
         nc.scalar.activation(out=warm_out[:], in_=warm[:], func=ACT.Sqrt)
+        load_xn(nc.scalar)
         nc.vector.transpose(out=cn_cols[:], in_=cn_rows[:])
+        repeat_cn(vcopy, 0, 0, 1)
+        repeat_cn(scopy, 0, 1, 2)
         interleave(scopy, x_bf[:], x_raw[:])
-        repeat_cn(vcopy, 0)
         repeat_cn(scopy, 1)
         spread_cn(0)
         quantize(x_codes, x_scales, x_bf)
-        spread_cn(1)
-        interleave_c(scopy, 0)
-        quantize_c(0)
+        interleave_c(vcopy, 0)
         interleave_c(scopy, 1)
-        interleave_c(vcopy, 2)
+        spread_cn(1, 0, 1)
+        quantize_c(0)
+        spread_cn(1, 1, 2)
         quantize_c(1)
+        interleave_c(vcopy, 2)
         interleave_c(scopy, 3)
-        squared(0, 0)
-        squared(0, 1)
+        squared(0, 0, 128)
         quantize_c(2)
         quantize_c(3)
+        squared(1, 0, 128)
+        roots(0, 128)
         for k in range(1, 4):
-            squared(k, 0)
-            squared(k, 1)
-        for g in range(G):
-            root(g, 0, 256)
-        for k in range(2, 4):
-            for g in range(G):
-                root(g, k * CHUNK, (k + 1) * CHUNK)
+            squares(k)
+            roots(k * CHUNK, (k + 1) * CHUNK)
         for g in range(G):
             for h in range(2):
                 finish(nc.sync, g, h * HALF, (h + 1) * HALF)

@@ -30,12 +30,12 @@ def tile_rows_kern_laplace_kernel(tc, x, c, xn, cn, out):
         ctx.enter_context(tc.manual_schedule())
 
         x_raw = sb.tile([P, PACK, M], F32, name="x_raw", align_bytes=64)
-        loads = [(0, 256), (256, 512)]
+        loads = [(0, 512)]
         c_raw = [sb.tile([P, PACK, hi - lo], F32, name="c_raw%d" % lo, align_bytes=64) for lo, hi in loads]
-        cn_rows = sb.tile([P, SQ], F32, name="cn_rows", align_bytes=64)
-        cn_cols = sb.tile([P, SQ], F32, name="cn_cols", align_bytes=64)
-        cn_rep = [sb.tile([P, G * HALF], F32, name="cn_rep%d" % h, align_bytes=64) for h in range(2)]
-        cn_all = [sb.tile([P, G * HALF], F32, name="cn_all%d" % h, align_bytes=64) for h in range(2)]
+        cn_rows = sb.tile([P, P], F32, name="cn_rows", align_bytes=64)
+        cn_cols = sb.tile([P, P], F32, name="cn_cols", align_bytes=64)
+        cn_rep = [sb.tile([P, N], F32, name="cn_rep%d" % g, align_bytes=64) for g in range(G)]
+        cn_all = [sb.tile([P, N], F32, name="cn_all%d" % g, align_bytes=64) for g in range(G)]
         xn_col = sb.tile([P, G], F32, name="xn_col")
         warm = sb.tile([P, 1], F32, name="warm")
         warm_out = sb.tile([P, 1], F32, name="warm_out")
@@ -68,7 +68,7 @@ def tile_rows_kern_laplace_kernel(tc, x, c, xn, cn, out):
         def load_cn(q):
             q.dma_start(
                 out=cn_rows[:],
-                in_=cn.rearrange("g o (b i) -> o (g b) i", i=SQ).to_broadcast([P // SQ, SQ, SQ]),
+                in_=cn.rearrange("g o (r i) -> o (g r) i", i=P).to_broadcast([P * P // (G * N), G * N // P, P]),
             )
 
         def load_xn(q):
@@ -103,23 +103,22 @@ def tile_rows_kern_laplace_kernel(tc, x, c, xn, cn, out):
                     stop=True,
                 )
 
-        def repeat_cn(copy, h, g0=0, g1=G):
-            per = HALF // SQ
+        def repeat_cn(copy, g, lo=0, hi=N):
+            r0, r1 = (g * N + lo) // P, (g * N + hi) // P
             copy(
-                out=cn_rep[h][:, g0 * HALF : g1 * HALF].rearrange("p (g b r) -> p g b r", b=per, r=SQ),
-                in_=cn_cols[:].rearrange("p (g h b) -> p g h b", g=G, h=2)[:, g0:g1, h, :].unsqueeze(3).to_broadcast([P, g1 - g0, per, SQ]),
+                out=cn_rep[g][:, lo:hi].rearrange("p (r b i) -> p r b i", b=P // SQ, i=SQ),
+                in_=cn_cols[:].rearrange("p (b r) -> p r b", r=SQ)[:, r0:r1, :].unsqueeze(3).to_broadcast([P, r1 - r0, P // SQ, SQ]),
             )
 
-        def spread_cn(h, g0=0, g1=G):
-            nc.vector.transpose(out=cn_all[h][:, g0 * HALF : g1 * HALF], in_=cn_rep[h][:, g0 * HALF : g1 * HALF])
+        def spread_cn(g, lo=0, hi=N):
+            nc.vector.transpose(out=cn_all[g][:, lo:hi], in_=cn_rep[g][:, lo:hi])
 
         def squared(g, lo, hi):
-            h, first = divmod(lo, HALF)
             nc.vector.scalar_tensor_tensor(
                 out=d2[:, g * N + lo : g * N + hi],
                 in0=z_view(g, lo, hi),
                 scalar=-2.0,
-                in1=cn_all[h][:, g * HALF + first : g * HALF + first + hi - lo],
+                in1=cn_all[g][:, lo:hi],
                 op0=ALU.mult,
                 op1=ALU.add,
             )
@@ -144,34 +143,31 @@ def tile_rows_kern_laplace_kernel(tc, x, c, xn, cn, out):
         vcopy = nc.vector.tensor_copy
         scopy = nc.scalar.copy
 
-        load_cn(nc.sync)
+        load_cn(nc.scalar)
         load_x(nc.sync)
-        for h in range(len(loads)):
-            load_c(nc.sync, h)
+        load_c(nc.sync, 0)
+        load_xn(nc.sync)
         nc.vector.memset(warm[:], 1.0)
         nc.scalar.activation(out=warm_out[:], in_=warm[:], func=ACT.Sqrt)
-        load_xn(nc.scalar)
         nc.vector.transpose(out=cn_cols[:], in_=cn_rows[:])
-        repeat_cn(vcopy, 0, 0, 1)
-        repeat_cn(scopy, 0, 1, 2)
-        interleave(scopy, x_bf[:], x_raw[:])
+        repeat_cn(vcopy, 0)
         repeat_cn(scopy, 1)
+        interleave(scopy, x_bf[:], x_raw[:])
         spread_cn(0)
+        spread_cn(1)
         quantize(x_codes, x_scales, x_bf)
-        interleave_c(vcopy, 0)
+        interleave_c(vcopy, 0, 0, 88)
+        interleave_c(scopy, 0, 88, 128)
         interleave_c(scopy, 1)
-        spread_cn(1, 0, 1)
+        interleave_c(vcopy, 2, 0, 64)
         quantize_c(0)
-        spread_cn(1, 1, 2)
+        interleave_c(vcopy, 2, 64, 128)
+        interleave_c(vcopy, 3, 0, 64)
+        interleave_c(scopy, 3, 64, 128)
         quantize_c(1)
-        interleave_c(vcopy, 2)
-        interleave_c(scopy, 3)
-        squared(0, 0, 128)
         quantize_c(2)
         quantize_c(3)
-        squared(1, 0, 128)
-        roots(0, 128)
-        for k in range(1, 4):
+        for k in range(4):
             squares(k)
             roots(k * CHUNK, (k + 1) * CHUNK)
         for g in range(G):

from contextlib import ExitStack

import concourse.mybir as mybir

G, D, M, N = 2, 256, 128, 512
FLOPS = 2 * G * D * M * N

F32 = mybir.dt.float32
BF16 = mybir.dt.bfloat16
U32 = mybir.dt.uint32
U8 = mybir.dt.uint8
FP8X4 = mybir.dt.float8_e4m3fn_x4
ACT = mybir.ActivationFunctionType
ALU = mybir.AluOpType

P = 128
PACK = 4
ROWS = D // PACK
SQ = 32
HALF = N // 2
CHUNK = 128
RUN = 2


def tile_rows_kern_laplace_kernel(tc, x, c, xn, cn, out):
    nc = tc.nc
    with ExitStack() as ctx:
        sb = ctx.enter_context(tc.tile_pool(name="sb", bufs=1))
        ps = ctx.enter_context(tc.psum_pool(name="ps", bufs=1))
        ctx.enter_context(tc.manual_schedule())

        x_raw = sb.tile([P, PACK, M], F32, name="x_raw", align_bytes=64)
        loads = [(0, 512)]
        c_raw = [sb.tile([P, PACK, hi - lo], F32, name="c_raw%d" % lo, align_bytes=64) for lo, hi in loads]
        cn_rows = sb.tile([P, P], F32, name="cn_rows", align_bytes=64)
        cn_cols = sb.tile([P, P], F32, name="cn_cols", align_bytes=64)
        cn_rep = [sb.tile([P, N], F32, name="cn_rep%d" % g, align_bytes=64) for g in range(G)]
        cn_all = [sb.tile([P, N], F32, name="cn_all%d" % g, align_bytes=64) for g in range(G)]
        xn_col = sb.tile([P, G], F32, name="xn_col")
        warm = sb.tile([P, 1], F32, name="warm")
        warm_out = sb.tile([P, 1], F32, name="warm_out")
        x_bf = sb.tile([P, M * PACK], BF16, name="x_bf", align_bytes=64)
        x_codes = sb.tile([P, M], U32, name="x_codes", align_bytes=64)
        x_scales = sb.tile([P, M], U8, name="x_scales", align_bytes=64)
        chunks = range(N // CHUNK)
        c_bf = [sb.tile([P, CHUNK * PACK], BF16, name="c_bf%d" % k, align_bytes=64) for k in chunks]
        c_codes = [sb.tile([P, CHUNK], U32, name="c_codes%d" % k, align_bytes=64) for k in chunks]
        c_scales = [sb.tile([P, CHUNK], U8, name="c_scales%d" % k, align_bytes=64) for k in chunks]
        spans = [(0, 128), (128, 256), (256, 384), (384, 512)]
        banks = [[ps.tile([P, hi - lo], F32, name="z%d_%d" % (g, lo)) for lo, hi in spans] for g in range(G)]

        def z_view(g, lo, hi):
            s = [i for i in range(len(spans)) if spans[i][0] <= lo < spans[i][1]][0]
            return banks[g][s][:, lo - spans[s][0] : hi - spans[s][0]]

        d2 = sb.tile([P, G * N], F32, name="d2", align_bytes=64)
        dist = sb.tile([P, G * N], F32, name="dist", align_bytes=64)
        y = sb.tile([P, G * N], F32, name="y", align_bytes=64)

        c_rows = c.rearrange("g (p j) n -> (g p) j n", j=PACK)

        def load_x(q):
            q.dma_start(out=x_raw[:], in_=x.rearrange("g (p j) m -> (g p) j m", j=PACK))

        def load_c(q, h):
            q.dma_start(out=c_raw[h][:], in_=c_rows[:, :, loads[h][0] : loads[h][1]])

        def load_cn(q):
            q.dma_start(
                out=cn_rows[:],
                in_=cn.rearrange("g o (r i) -> o (g r) i", i=P).to_broadcast([P * P // (G * N), G * N // P, P]),
            )

        def load_xn(q):
            with nc.allow_non_contiguous_dma(reason="one squared length a partition"):
                q.dma_start(out=xn_col[:], in_=xn.rearrange("g m o -> m (g o)"))

        def interleave(copy, dst, src):
            copy(
                out=dst.rearrange("p (w i t) -> p w t i", i=RUN, t=PACK),
                in_=src.rearrange("p t (w i) -> p w t i", i=RUN),
            )

        def interleave_c(copy, k, lo=0, hi=CHUNK):
            h = [i for i in range(len(loads)) if loads[i][0] <= k * CHUNK < loads[i][1]][0]
            first = k * CHUNK - loads[h][0]
            interleave(copy, c_bf[k][:, lo * PACK : hi * PACK], c_raw[h][:, :, first + lo : first + hi])

        def quantize(codes, scales, src):
            nc.vector.quantize_mx(out=codes[:].bitcast(FP8X4), scales=scales[:], in_=src[:])

        def quantize_c(k):
            quantize(c_codes[k], c_scales[k], c_bf[k])
            for g in range(G):
                rows = slice(g * ROWS, (g + 1) * ROWS)
                nc.tensor.matmul_mx(
                    out=z_view(g, k * CHUNK, (k + 1) * CHUNK),
                    lhsT=x_codes[rows, :].bitcast(FP8X4),
                    lhsT_scale=x_scales[rows, :],
                    rhs=c_codes[k][rows, :].bitcast(FP8X4),
                    rhs_scale=c_scales[k][rows, :],
                    start=True,
                    stop=True,
                )

        def repeat_cn(copy, g, lo=0, hi=N):
            r0, r1 = (g * N + lo) // P, (g * N + hi) // P
            copy(
                out=cn_rep[g][:, lo:hi].rearrange("p (r b i) -> p r b i", b=P // SQ, i=SQ),
                in_=cn_cols[:].rearrange("p (b r) -> p r b", r=SQ)[:, r0:r1, :].unsqueeze(3).to_broadcast([P, r1 - r0, P // SQ, SQ]),
            )

        def spread_cn(g, lo=0, hi=N):
            nc.vector.transpose(out=cn_all[g][:, lo:hi], in_=cn_rep[g][:, lo:hi])

        def squared(g, lo, hi):
            nc.vector.scalar_tensor_tensor(
                out=d2[:, g * N + lo : g * N + hi],
                in0=z_view(g, lo, hi),
                scalar=-2.0,
                in1=cn_all[g][:, lo:hi],
                op0=ALU.mult,
                op1=ALU.add,
            )

        def root(g, lo, hi):
            cols = slice(g * N + lo, g * N + hi)
            nc.scalar.activation(out=dist[:, cols], in_=d2[:, cols], func=ACT.Sqrt, bias=xn_col[:, g : g + 1])

        def finish(q, g, lo, hi):
            cols = slice(g * N + lo, g * N + hi)
            nc.scalar.activation(out=y[:, cols], in_=dist[:, cols], func=ACT.Exp, scale=-1.5)
            q.dma_start(out=out[g, :, lo:hi], in_=y[:, cols])

        def squares(k):
            for g in range(G):
                squared(g, k * CHUNK, (k + 1) * CHUNK)

        def roots(lo, hi):
            for g in range(G):
                root(g, lo, hi)

        vcopy = nc.vector.tensor_copy
        scopy = nc.scalar.copy

        load_cn(nc.scalar)
        load_x(nc.sync)
        load_c(nc.sync, 0)
        load_xn(nc.sync)
        nc.vector.memset(warm[:], 1.0)
        nc.scalar.activation(out=warm_out[:], in_=warm[:], func=ACT.Sqrt)
        nc.vector.transpose(out=cn_cols[:], in_=cn_rows[:])
        repeat_cn(vcopy, 0)
        repeat_cn(scopy, 1)
        interleave(scopy, x_bf[:], x_raw[:])
        spread_cn(0)
        spread_cn(1)
        quantize(x_codes, x_scales, x_bf)
        interleave_c(vcopy, 0, 0, 88)
        interleave_c(scopy, 0, 88, 128)
        interleave_c(scopy, 1)
        interleave_c(vcopy, 2, 0, 64)
        quantize_c(0)
        interleave_c(vcopy, 2, 64, 128)
        interleave_c(vcopy, 3, 0, 64)
        interleave_c(scopy, 3, 64, 128)
        quantize_c(1)
        quantize_c(2)
        quantize_c(3)
        for k in range(4):
            squares(k)
            roots(k * CHUNK, (k + 1) * CHUNK)
        for g in range(G):
            for h in range(2):
                finish(nc.sync, g, h * HALF, (h + 1) * HALF)
